import numpy as np
import ml_dtypes


def mxq(x, axis, fmt="e4m3"):
    dtype, down = {"e4m3": (ml_dtypes.float8_e4m3fn, 7), "e5m2": (ml_dtypes.float8_e5m2, 14)}[fmt]
    v = np.moveaxis(np.asarray(x, np.float32).astype(ml_dtypes.bfloat16).astype(np.float64), axis, -1)
    blocks = v.reshape(v.shape[:-1] + (-1, 32))
    amax = np.abs(blocks).max(-1, keepdims=True)
    byte = np.maximum(np.where(amax > 0, np.frexp(amax)[1] - 1 + 127, 0) - down, 1)
    scale = np.exp2(byte - 127.0)
    codes = (blocks / scale).astype(np.float32).astype(dtype).astype(np.float64)
    return np.moveaxis((codes * scale).reshape(v.shape), -1, axis)


WIDE = False


def mx_kscale(k):
    if not WIDE:
        return np.ones(k)
    levels = np.array([18, -18])
    if k % 512:
        return np.exp2(np.random.permutation(np.resize(levels, k // 32))).repeat(32)
    a = np.empty((k // 512, 16))
    for p in range(k // 512):
        a[p, :8] = np.random.permutation(np.resize(levels, 8))
        for g in range(8):
            far = levels[np.abs(levels - a[p, g]) >= 10]
            a[p, g + 8] = far[np.random.randint(len(far))]
    return np.exp2(a.ravel()).repeat(32)


def f64(x):
    return np.asarray(x).astype(np.float64)


def striped(idx):
    return np.tile(np.asarray(idx).reshape(-1, 16).T, (8, 1)).astype(np.uint16)


def unstriped(offs):
    return offs[:16].T.reshape(-1).astype(np.int64)


E2M1 = np.array([0.0, 0.5, 1.0, 1.5, 2.0, 3.0, 4.0, 6.0, -0.0, -0.5, -1.0, -1.5, -2.0, -3.0, -4.0, -6.0])


def pack_weight(w, fmt):
    k, n = w.shape
    w = f64(np.asarray(w, np.float32).astype(ml_dtypes.bfloat16)).reshape(k // 32, 32, n)
    amax = np.abs(w).max(1)
    if fmt == "e4m3":
        byte = np.frexp(amax)[1] - 1 + 127 - 7
    else:
        mant, ex = np.frexp(amax / 6.0)
        byte = np.where(mant > 0.5, ex, ex - 1) + 127
    byte = np.clip(np.where(amax > 0, byte, 1), 1, 254)
    scaled = (w * np.exp2(127.0 - byte)[:, None, :]).reshape(k, n).astype(np.float32)
    by_word = np.ascontiguousarray(scaled.reshape(k // 512, 128, 4, n).transpose(0, 1, 3, 2))
    if fmt == "e4m3":
        words = by_word.astype(ml_dtypes.float8_e4m3fn).view(np.uint8)
    else:
        c = by_word.astype(ml_dtypes.float4_e2m1fn).view(np.uint8) & 0xF
        words = (c[..., 0::2] | (c[..., 1::2] << 4)).reshape(k // 512, 128, 2 * n)
    return np.ascontiguousarray(words), np.ascontiguousarray(byte.astype(np.uint8).reshape(k // 512, 16, n))


def unpack_weight(words, scales, fmt):
    g, _, n = scales.shape
    words = np.ascontiguousarray(words).reshape(g, 128, n, -1)
    if fmt == "e4m3":
        vals = words.view(ml_dtypes.float8_e4m3fn).astype(np.float64)
    else:
        nib = np.empty((g, 128, n, 4), np.uint8)
        nib[..., 0::2] = words & 0xF
        nib[..., 1::2] = words >> 4
        vals = E2M1[nib]
    vals = vals * np.repeat(np.exp2(scales.astype(np.float64) - 127.0), 8, axis=1)[..., None]
    return vals.transpose(0, 1, 3, 2).reshape(g * 512, n)


T, C, D, DV = 1024, 2048, 512, 512
BETA = 0.25


def setup_inputs():
    n = np.random.standard_normal
    grid = lambda v: np.clip(np.round(v * 16) / 16, -4, 4)
    v = mx_kscale(DV)[:, None]
    wp = pack_weight(n((DV, D)) / np.sqrt(DV) / v, "e4m3")
    return {
        "zT": (grid(n((DV, T))) * v).astype(np.float32),
        "cb": (grid(n((DV, C))) * v).astype(np.float32),
        "dyT": (grid(0.5 * n((DV, T))) * v).astype(np.float32),
        "tw": np.tile(np.random.randint(8, 33, T) / 16.0, (128, 1)).astype(np.float32),
        "w_words": wp[0],
        "w_scales": wp[1],
        "offs": striped(np.random.randint(0, C, T)),
    }


def reference(zT, cb, dyT, tw, w_words, w_scales, offs):
    e = f64(zT) - f64(cb)[:, unstriped(offs)]
    g = f64(tw)[:1] * (f64(dyT) + BETA * e)
    return unpack_weight(w_words, w_scales, "e4m3").T @ mxq(g, 0, "e5m2")

@@ -1,0 +1,179 @@
+from contextlib import ExitStack
+
+import concourse.mybir as mybir
+from concourse.masks import make_identity
+
+T, C, D, DV = 1024, 2048, 512, 512
+BETA = 0.25
+FLOPS = 2 * DV * D * T
+BYTES = 4 * (2 * DV * T + DV * C + T + D * T) + DV * D + 16 * D + 128 * (T // 16) * 2
+
+F32 = mybir.dt.float32
+BF16 = mybir.dt.bfloat16
+I32 = mybir.dt.int32
+U32 = mybir.dt.uint32
+U16 = mybir.dt.uint16
+U8 = mybir.dt.uint8
+E4M3X4 = mybir.dt.float8_e4m3fn_x4
+E5M2X4 = mybir.dt.float8_e5m2_x4
+MULT = mybir.AluOpType.mult
+ADD = mybir.AluOpType.add
+COPY = mybir.ActivationFunctionType.Copy
+
+P = 128
+LANES = 4
+HALF = 512
+PAIR = 256
+HALVES = T // HALF
+TURNED = (3, 2)
+PIECES = ((slice(384, 512),), (slice(256, 384), slice(384, 512)))
+SCALE_ON_VECTOR = (2,)
+BACK = (((0, 2, False), (2, 1, True)), ((0, 2, False),))
+TWO = (slice(0, 2), slice(2, 4))
+LAST = (slice(0, 2), slice(2, 3), slice(3, 4))
+LOADS = ((TWO, LAST), (TWO, LAST))
+
+
+def tile_attend_gvq_sw_x_kernel(tc, zT, cb, dyT, tw, w_words, w_scales, offs, out):
+    nc = tc.nc
+    with ExitStack() as ctx:
+        keep = ctx.enter_context(tc.tile_pool(name="keep", bufs=1))
+        psum = ctx.enter_context(tc.psum_pool(name="psum", bufs=8))
+
+        offsets = keep.tile([P, T // 16], U16, name="offsets")
+        nc.sync.dma_start(offsets[:], offs)
+
+        cb_lanes = cb.rearrange("(p j) c -> p j c", j=LANES)
+        z_lanes = zT.rearrange("(p j) t -> p j t", j=LANES)
+        dy_lanes = dyT.rearrange("(p j) t -> p j t", j=LANES)
+
+        book = [keep.tile([P, C], F32, name="book%d" % j) for j in range(LANES)]
+        z = [keep.tile([P, LANES, HALF], F32, name="z%d" % h) for h in range(HALVES)]
+        dy = [keep.tile([P, LANES, HALF], F32, name="dy%d" % h) for h in range(HALVES)]
+        w_code = keep.tile([P, D], U32, name="w_code", align_bytes=64)
+
+        tw_rows = keep.tile([P, P], F32, name="tw_rows")
+        nc.gpsimd.memset(tw_rows[:], 0.0)
+        for j in range(LANES):
+            nc.sync.dma_start(book[j][:], cb_lanes[:, j, :])
+            if j == 0:
+                nc.sync.dma_start(tw_rows[0 : T // P, :], tw[0].rearrange("(b c) -> b c", c=P))
+        for h in range(HALVES):
+            for src, dst in ((z_lanes, z[h]), (dy_lanes, dy[h])):
+                for lanes in LOADS[h][0 if dst is z[h] else 1]:
+                    nc.sync.dma_start(dst[:, lanes, :], src[:, lanes, h * HALF : (h + 1) * HALF])
+            if h == 0:
+                nc.sync.dma_start(w_code[:].bitcast(I32), w_words[0].rearrange("p n t -> p (n t)").bitcast(I32))
+
+        ident = keep.tile([P, P], F32, name="ident")
+        make_identity(nc, ident[:])
+        minus_beta = keep.tile([P, HALF], F32, name="minus_beta")
+        nc.vector.memset(minus_beta[:], -BETA)
+
+        w_scale = keep.tile([P, D], U8, name="w_scale", align_bytes=64)
+        nc.gpsimd.memset(w_scale[:].bitcast(I32), 0)
+        for q in range(4):
+            nc.scalar.dma_start(w_scale[32 * q : 32 * q + 4, :].bitcast(I32), w_scales[0, 4 * q : 4 * q + 4, :].bitcast(I32))
+
+        tw_bank = psum.tile([P, 4, P], F32, name="bank")
+        nc.tensor.transpose(tw_bank[:, 0, :], tw_rows[:], ident[:])
+        tw_cols = keep.tile([P, T // P], F32, name="tw_cols")
+        nc.scalar.activation(tw_cols[:], tw_bank[:, 0, 0 : T // P], COPY)
+        tw_wide = []
+        for h in range(HALVES):
+            spread = psum.tile([P, HALF], F32, name="bank")
+            for b in range(TURNED[h], HALF // P):
+                block = 4 * h + b
+                nc.tensor.transpose(spread[:, b * P : (b + 1) * P], tw_cols[:, block : block + 1].to_broadcast([P, P]), ident[:])
+            wide = keep.tile([P, HALF], F32, name="tw_wide%d" % h)
+            nc.scalar.copy(wide[:, TURNED[h] * P :], spread[:, TURNED[h] * P :])
+            tw_wide.append(wide)
+
+        loss = [keep.tile([P, LANES, HALF], F32, name="loss%d" % h) for h in range(HALVES)]
+        g_in = [keep.tile([P, HALF, LANES], BF16, name="g_in%d" % h, align_bytes=64) for h in range(HALVES)]
+        g_code = [keep.tile([P, HALF], U32, name="g_code%d" % h, align_bytes=64) for h in range(HALVES)]
+        g_scale = [keep.tile([P, HALF], U8, name="g_scale%d" % h, align_bytes=64) for h in range(HALVES)]
+        cols = HALF // 16
+
+        def add_turned(bank, j, block, start, stop):
+            nc.tensor.matmul(bank[:, j, :], block, ident[:], start=start, stop=stop, is_transpose=True)
+
+        def quantise(h, tok):
+            nc.vector.quantize_mx(
+                out=g_code[h][:, tok].bitcast(E5M2X4), scales=g_scale[h][:, tok],
+                in_=g_in[h][:, tok, :].rearrange("p t j -> p (t j)"),
+            )
+
+        sums = [[psum.tile([P, LANES, P], F32, name="bank") for b in range(TURNED[h])] for h in range(HALVES)]
+        for j in range(LANES):
+            for h in range(HALVES):
+                nc.vector.tensor_tensor(
+                    loss[h][:, j, :], book[j][:].indirect(offsets[:, h * cols : (h + 1) * cols]), minus_beta[:], MULT
+                )
+                for b in range(TURNED[h]):
+                    add_turned(sums[h][b], j, loss[h][:, j, b * P : (b + 1) * P], j == 0, False)
+
+        def form(h):
+            n = TURNED[h]
+            turned, direct = slice(0, n * P), slice(n * P, HALF)
+            for lanes in LOADS[h][0]:
+                nc.scalar.activation(z[h][:, lanes, turned], z[h][:, lanes, turned], COPY, scale=BETA)
+                nc.vector.scalar_tensor_tensor(loss[h][:, lanes, direct], z[h][:, lanes, direct], BETA, loss[h][:, lanes, direct], MULT, ADD)
+                for j in range(lanes.start, lanes.stop):
+                    for b in range(n):
+                        add_turned(sums[h][b], j, z[h][:, j, b * P : (b + 1) * P], False, False)
+            for lanes in LOADS[h][1]:
+                for j in range(lanes.start, lanes.stop):
+                    for b in range(n):
+                        add_turned(sums[h][b], j, dy[h][:, j, b * P : (b + 1) * P], False, j == LANES - 1)
+                nc.vector.tensor_tensor(loss[h][:, lanes, direct], loss[h][:, lanes, direct], dy[h][:, lanes, direct], ADD)
+            g_rows = []
+            for b in range(n):
+                block = 4 * h + b
+                rows = keep.tile([P, 2, P, 2], BF16, name="g_rows%d" % block)
+                g_rows.append(rows)
+                src = sums[h][b][:].rearrange("t (u e) p -> t u p e", e=2)
+                if block in SCALE_ON_VECTOR:
+                    nc.vector.tensor_scalar(rows[:], src, tw_cols[:, block : block + 1], None, MULT)
+                else:
+                    nc.scalar.activation(rows[:], src, COPY, scale=tw_cols[:, block : block + 1])
+            for first, count, on_vector in BACK[h]:
+                back = psum.tile([P, 4, P], F32, name="bank")
+                for b in range(count):
+                    words = g_rows[first + b][:].rearrange("t u p e -> t (u p e)").bitcast(F32)
+                    for u in range(2):
+                        nc.tensor.transpose(back[:, 2 * b + u, :], words[:, u * P : (u + 1) * P], ident[:])
+                tok = slice(first * P, (first + count) * P)
+                copy = nc.vector.tensor_copy if on_vector else nc.scalar.copy
+                copy(
+                    g_in[h][:, tok, :].rearrange("p t j -> p (t j)").bitcast(F32).rearrange("p (b t u) -> p b t u", b=count, u=2),
+                    back[:, 0 : 2 * count, :].rearrange("p (b u) t -> p b t u", u=2),
+                )
+            for tok in PIECES[h]:
+                nc.vector.tensor_tensor(
+                    g_in[h][:, tok, :], loss[h][:, :, tok].rearrange("p j t -> p t j"),
+                    tw_wide[h][:, tok].unsqueeze(2).to_broadcast([P, tok.stop - tok.start, LANES]), MULT,
+                )
+            for tok in PIECES[h]:
+                quantise(h, tok)
+            for first, count, on_vector in BACK[h]:
+                quantise(h, slice(first * P, (first + count) * P))
+
+        def multiply(h):
+            for m in range(D // P):
+                acc = psum.tile([P, HALF], F32, name="bank")
+                ch = slice(m * P, (m + 1) * P)
+                nc.tensor.matmul_mx(
+                    out=acc[:], lhsT=w_code[:, ch].bitcast(E4M3X4), lhsT_scale=w_scale[:, ch],
+                    rhs=g_code[h][:].bitcast(E5M2X4), rhs_scale=g_scale[h][:], start=True, stop=True,
+                )
+                res = keep.tile([P, HALF], F32, name="res%d_%d" % (h, m))
+                if h == HALVES - 1 and m % 2 == 1:
+                    nc.vector.tensor_copy(res[:], acc[:])
+                else:
+                    nc.scalar.copy(res[:], acc[:])
+                nc.sync.dma_start(out[ch, h * HALF : (h + 1) * HALF], res[:])
+
+        for h in range(HALVES):
+            form(h)
+            multiply(h)

@@ -25,13 +25,18 @@ LANES = 4
 HALF = 512
 PAIR = 256
 HALVES = T // HALF
-TURNED = (3, 2)
-PIECES = ((slice(384, 512),), (slice(256, 384), slice(384, 512)))
-SCALE_ON_VECTOR = (2,)
-BACK = (((0, 2, False), (2, 1, True)), ((0, 2, False),))
-TWO = (slice(0, 2), slice(2, 4))
-LAST = (slice(0, 2), slice(2, 3), slice(3, 4))
-LOADS = ((TWO, LAST), (TWO, LAST))
+LOADS = [('cb', 1, 0, 0, 0), ('cb', 0, 0, 0, 0), ('cb', 3, 0, 0, 0), ('z', 0, 2, 0, 8), ('tw', 0, 0, 0, 0), ('ws', 0, 0, 0, 0), ('cb', 2, 0, 0, 0), ('z', 2, 4, 0, 8), ('dy', 2, 3, 0, 4), ('dy', 3, 4, 0, 3), ('dy', 0, 2, 0, 4), ('dy', 3, 4, 3, 6), ('dy', 1, 3, 4, 5), ('dy', 0, 1, 4, 6), ('dy', 1, 3, 5, 6), ('dy', 0, 2, 6, 8), ('dy', 2, 4, 6, 8), ('w', 0, 0, 0, 0)]
+STEPS = [('g', 1, 2, 0, 4), ('g', 1, 2, 4, 8), ('g', 0, 1, 0, 4), ('g', 0, 1, 4, 8), ('g', 3, 4, 0, 4), ('g', 2, 3, 0, 4), ('g', 3, 4, 4, 8), ('z', 0, 2, 0, 8), ('g', 2, 3, 4, 8), ('z', 2, 4, 0, 8), ('dy', 2, 3, 0, 4), ('dy', 3, 4, 0, 3), ('dy', 0, 2, 0, 4), ('dy', 3, 4, 3, 6), ('dy', 1, 3, 4, 5), ('mm', 0, 0, 0, 0), ('dy', 0, 1, 4, 6), ('dy', 1, 3, 5, 6), ('dy', 0, 2, 6, 8), ('dy', 2, 4, 6, 8), ('mm', 1, 0, 0, 0)]
+ROAD = 'VVZZSSVV'
+SCALE = 'SVSSSSVS'
+BACK = 'VVSSSSVS'
+EMPTY = 'SSSSVSVS'
+EARLY = [3, 5]
+GIN = [1, 2, 0, 3, 4, 7, 3, 3]
+GROWS = [4, 4, 2, 5, 7, 0, 3, 5]
+MULW = 2
+ADDW = 4
+BACKW = 2
 
 
 def tile_attend_gvq_sw_x_kernel(tc, zT, cb, dyT, tw, w_words, w_scales, offs, out):
@@ -44,136 +49,173 @@ def tile_attend_gvq_sw_x_kernel(tc, zT, cb, dyT, tw, w_words, w_scales, offs, ou
         nc.sync.dma_start(offsets[:], offs)
 
         cb_lanes = cb.rearrange("(p j) c -> p j c", j=LANES)
-        z_lanes = zT.rearrange("(p j) t -> p j t", j=LANES)
-        dy_lanes = dyT.rearrange("(p j) t -> p j t", j=LANES)
-
+        lanes_of = {"z": zT.rearrange("(p j) t -> p j t", j=LANES), "dy": dyT.rearrange("(p j) t -> p j t", j=LANES)}
         book = [keep.tile([P, C], F32, name="book%d" % j) for j in range(LANES)]
-        z = [keep.tile([P, LANES, HALF], F32, name="z%d" % h) for h in range(HALVES)]
-        dy = [keep.tile([P, LANES, HALF], F32, name="dy%d" % h) for h in range(HALVES)]
+        held = {"z": keep.tile([P, LANES, T], F32, name="z"), "dy": keep.tile([P, LANES, T], F32, name="dy")}
+        z, dy = held["z"], held["dy"]
         w_code = keep.tile([P, D], U32, name="w_code", align_bytes=64)
-
+        w_scale = keep.tile([P, D], U8, name="w_scale", align_bytes=64)
         tw_rows = keep.tile([P, P], F32, name="tw_rows")
         nc.gpsimd.memset(tw_rows[:], 0.0)
-        for j in range(LANES):
-            nc.sync.dma_start(book[j][:], cb_lanes[:, j, :])
-            if j == 0:
+        nc.gpsimd.memset(w_scale[:].bitcast(I32), 0)
+
+        for what, j0, j1, b0, b1 in LOADS:
+            if what == "cb":
+                nc.sync.dma_start(book[j0][:], cb_lanes[:, j0, :])
+            elif what == "tw":
                 nc.sync.dma_start(tw_rows[0 : T // P, :], tw[0].rearrange("(b c) -> b c", c=P))
-        for h in range(HALVES):
-            for src, dst in ((z_lanes, z[h]), (dy_lanes, dy[h])):
-                for lanes in LOADS[h][0 if dst is z[h] else 1]:
-                    nc.sync.dma_start(dst[:, lanes, :], src[:, lanes, h * HALF : (h + 1) * HALF])
-            if h == 0:
+            elif what == "w":
                 nc.sync.dma_start(w_code[:].bitcast(I32), w_words[0].rearrange("p n t -> p (n t)").bitcast(I32))
+            elif what == "ws":
+                for q in range(4):
+                    nc.scalar.dma_start(w_scale[32 * q : 32 * q + 4, :].bitcast(I32), w_scales[0, 4 * q : 4 * q + 4, :].bitcast(I32))
+            else:
+                nc.sync.dma_start(held[what][:, j0:j1, b0 * P : b1 * P], lanes_of[what][:, j0:j1, b0 * P : b1 * P])
 
         ident = keep.tile([P, P], F32, name="ident")
         make_identity(nc, ident[:])
         minus_beta = keep.tile([P, HALF], F32, name="minus_beta")
         nc.vector.memset(minus_beta[:], -BETA)
 
-        w_scale = keep.tile([P, D], U8, name="w_scale", align_bytes=64)
-        nc.gpsimd.memset(w_scale[:].bitcast(I32), 0)
-        for q in range(4):
-            nc.scalar.dma_start(w_scale[32 * q : 32 * q + 4, :].bitcast(I32), w_scales[0, 4 * q : 4 * q + 4, :].bitcast(I32))
-
         tw_bank = psum.tile([P, 4, P], F32, name="bank")
         nc.tensor.transpose(tw_bank[:, 0, :], tw_rows[:], ident[:])
         tw_cols = keep.tile([P, T // P], F32, name="tw_cols")
         nc.scalar.activation(tw_cols[:], tw_bank[:, 0, 0 : T // P], COPY)
-        tw_wide = []
-        for h in range(HALVES):
-            spread = psum.tile([P, HALF], F32, name="bank")
-            for b in range(TURNED[h], HALF // P):
-                block = 4 * h + b
-                nc.tensor.transpose(spread[:, b * P : (b + 1) * P], tw_cols[:, block : block + 1].to_broadcast([P, P]), ident[:])
-            wide = keep.tile([P, HALF], F32, name="tw_wide%d" % h)
-            nc.scalar.copy(wide[:, TURNED[h] * P :], spread[:, TURNED[h] * P :])
-            tw_wide.append(wide)
+        tw_wide = keep.tile([P, T], F32, name="tw_wide")
+        direct = [b for b in range(T // P) if ROAD[b] == "V"]
+        for k in range(0, len(direct), 4):
+            spread = psum.tile([P, 4, P], F32, name="bank")
+            for i, b in enumerate(direct[k : k + 4]):
+                nc.tensor.transpose(spread[:, i, :], tw_cols[:, b : b + 1].to_broadcast([P, P]), ident[:])
+            for i, b in enumerate(direct[k : k + 4]):
+                nc.scalar.copy(tw_wide[:, b * P : (b + 1) * P], spread[:, i, :])
 
-        loss = [keep.tile([P, LANES, HALF], F32, name="loss%d" % h) for h in range(HALVES)]
-        g_in = [keep.tile([P, HALF, LANES], BF16, name="g_in%d" % h, align_bytes=64) for h in range(HALVES)]
-        g_code = [keep.tile([P, HALF], U32, name="g_code%d" % h, align_bytes=64) for h in range(HALVES)]
-        g_scale = [keep.tile([P, HALF], U8, name="g_scale%d" % h, align_bytes=64) for h in range(HALVES)]
+        loss = keep.tile([P, LANES, T], F32, name="loss")
+        g_code = keep.tile([P, T], U32, name="g_code", align_bytes=64)
+        g_scale = keep.tile([P, T], U8, name="g_scale", align_bytes=64)
         cols = HALF // 16
+        sums, turns = {}, {}
 
-        def add_turned(bank, j, block, start, stop):
-            nc.tensor.matmul(bank[:, j, :], block, ident[:], start=start, stop=stop, is_transpose=True)
+        def add_turned(b, j, source):
+            if b not in sums:
+                sums[b] = psum.tile([P, LANES, P], F32, name="bank")
+                turns[b] = 0
+            turns[b] += 1
+            total = (2 if ROAD[b] == "E" else 3) * LANES
+            nc.tensor.matmul(sums[b][:, j, :], source[:, j, b * P : (b + 1) * P], ident[:], start=(turns[b] == 1), stop=(turns[b] == total), is_transpose=True)
 
-        def quantise(h, tok):
-            nc.vector.quantize_mx(
-                out=g_code[h][:, tok].bitcast(E5M2X4), scales=g_scale[h][:, tok],
-                in_=g_in[h][:, tok, :].rearrange("p t j -> p (t j)"),
-            )
+        def quantise(g_in, b0, b1):
+            tok = slice(b0 * P, b1 * P)
+            nc.vector.quantize_mx(out=g_code[:, tok].bitcast(E5M2X4), scales=g_scale[:, tok], in_=g_in[:].rearrange("p t j -> p (t j)"))
 
-        sums = [[psum.tile([P, LANES, P], F32, name="bank") for b in range(TURNED[h])] for h in range(HALVES)]
-        for j in range(LANES):
-            for h in range(HALVES):
-                nc.vector.tensor_tensor(
-                    loss[h][:, j, :], book[j][:].indirect(offsets[:, h * cols : (h + 1) * cols]), minus_beta[:], MULT
-                )
-                for b in range(TURNED[h]):
-                    add_turned(sums[h][b], j, loss[h][:, j, b * P : (b + 1) * P], j == 0, False)
+        def runs(b0, b1, kinds, most):
+            found = []
+            for b in range(b0, b1):
+                if ROAD[b] in kinds:
+                    if found and found[-1][1] == b and b - found[-1][0] < most:
+                        found[-1][1] = b + 1
+                    else:
+                        found.append([b, b + 1])
+            return found
 
-        def form(h):
-            n = TURNED[h]
-            turned, direct = slice(0, n * P), slice(n * P, HALF)
-            for lanes in LOADS[h][0]:
-                nc.scalar.activation(z[h][:, lanes, turned], z[h][:, lanes, turned], COPY, scale=BETA)
-                nc.vector.scalar_tensor_tensor(loss[h][:, lanes, direct], z[h][:, lanes, direct], BETA, loss[h][:, lanes, direct], MULT, ADD)
-                for j in range(lanes.start, lanes.stop):
-                    for b in range(n):
-                        add_turned(sums[h][b], j, z[h][:, j, b * P : (b + 1) * P], False, False)
-            for lanes in LOADS[h][1]:
-                for j in range(lanes.start, lanes.stop):
-                    for b in range(n):
-                        add_turned(sums[h][b], j, dy[h][:, j, b * P : (b + 1) * P], False, j == LANES - 1)
-                nc.vector.tensor_tensor(loss[h][:, lanes, direct], loss[h][:, lanes, direct], dy[h][:, lanes, direct], ADD)
-            g_rows = []
-            for b in range(n):
-                block = 4 * h + b
-                rows = keep.tile([P, 2, P, 2], BF16, name="g_rows%d" % block)
-                g_rows.append(rows)
-                src = sums[h][b][:].rearrange("t (u e) p -> t u p e", e=2)
-                if block in SCALE_ON_VECTOR:
-                    nc.vector.tensor_scalar(rows[:], src, tw_cols[:, block : block + 1], None, MULT)
-                else:
-                    nc.scalar.activation(rows[:], src, COPY, scale=tw_cols[:, block : block + 1])
-            for first, count, on_vector in BACK[h]:
+        def finish(b0, b1):
+            g_rows = {}
+            for b in range(b0, b1):
+                if ROAD[b] != "V":
+                    g_rows[b] = keep.tile([P, 2, P, 2], BF16, name="g_rows%d" % GROWS[b])
+                    src = sums[b][:].rearrange("t (u e) p -> t u p e", e=2)
+                    if SCALE[b] == "V":
+                        nc.vector.tensor_scalar(g_rows[b][:], src, tw_cols[:, b : b + 1], None, MULT)
+                    else:
+                        nc.scalar.activation(g_rows[b][:], src, COPY, scale=tw_cols[:, b : b + 1])
+            made = []
+            for r0, r1 in runs(b0, b1, "V", 2):
+                g_in = keep.tile([P, (r1 - r0) * P, LANES], BF16, name="g_in%d" % GIN[r0], align_bytes=64)
+                made.append((g_in, r0, r1))
+                for s0, s1 in runs(r0, r1, "V", MULW):
+                    tok = slice(s0 * P, s1 * P)
+                    nc.vector.tensor_tensor(
+                        g_in[:, (s0 - r0) * P : (s1 - r0) * P, :], loss[:, :, tok].rearrange("p j t -> p t j"),
+                        tw_wide[:, tok].unsqueeze(2).to_broadcast([P, (s1 - s0) * P, LANES]), MULT,
+                    )
+            for g_in, r0, r1 in made:
+                quantise(g_in, r0, r1)
+            for r0, r1 in runs(b0, b1, "ESZ", BACKW):
                 back = psum.tile([P, 4, P], F32, name="bank")
-                for b in range(count):
-                    words = g_rows[first + b][:].rearrange("t u p e -> t (u p e)").bitcast(F32)
+                for b in range(r0, r1):
+                    words = g_rows[b][:].rearrange("t u p e -> t (u p e)").bitcast(F32)
                     for u in range(2):
-                        nc.tensor.transpose(back[:, 2 * b + u, :], words[:, u * P : (u + 1) * P], ident[:])
-                tok = slice(first * P, (first + count) * P)
-                copy = nc.vector.tensor_copy if on_vector else nc.scalar.copy
+                        nc.tensor.transpose(back[:, 2 * (b - r0) + u, :], words[:, u * P : (u + 1) * P], ident[:])
+                g_in = keep.tile([P, (r1 - r0) * P, LANES], BF16, name="g_in%d" % GIN[r0], align_bytes=64)
+                copy = nc.vector.tensor_copy if BACK[r0] == "V" else nc.scalar.copy
                 copy(
-                    g_in[h][:, tok, :].rearrange("p t j -> p (t j)").bitcast(F32).rearrange("p (b t u) -> p b t u", b=count, u=2),
-                    back[:, 0 : 2 * count, :].rearrange("p (b u) t -> p b t u", u=2),
+                    g_in[:].rearrange("p t j -> p (t j)").bitcast(F32).rearrange("p (b t u) -> p b t u", b=r1 - r0, u=2),
+                    back[:, 0 : 2 * (r1 - r0), :].rearrange("p (b u) t -> p b t u", u=2),
                 )
-            for tok in PIECES[h]:
-                nc.vector.tensor_tensor(
-                    g_in[h][:, tok, :], loss[h][:, :, tok].rearrange("p j t -> p t j"),
-                    tw_wide[h][:, tok].unsqueeze(2).to_broadcast([P, tok.stop - tok.start, LANES]), MULT,
-                )
-            for tok in PIECES[h]:
-                quantise(h, tok)
-            for first, count, on_vector in BACK[h]:
-                quantise(h, slice(first * P, (first + count) * P))
+                quantise(g_in, r0, r1)
 
         def multiply(h):
+            tok = slice(h * HALF, (h + 1) * HALF)
             for m in range(D // P):
                 acc = psum.tile([P, HALF], F32, name="bank")
                 ch = slice(m * P, (m + 1) * P)
                 nc.tensor.matmul_mx(
                     out=acc[:], lhsT=w_code[:, ch].bitcast(E4M3X4), lhsT_scale=w_scale[:, ch],
-                    rhs=g_code[h][:].bitcast(E5M2X4), rhs_scale=g_scale[h][:], start=True, stop=True,
+                    rhs=g_code[:, tok].bitcast(E5M2X4), rhs_scale=g_scale[:, tok], start=True, stop=True,
                 )
                 res = keep.tile([P, HALF], F32, name="res%d_%d" % (h, m))
-                if h == HALVES - 1 and m % 2 == 1:
+                if EMPTY[4 * h + m] == "V":
                     nc.vector.tensor_copy(res[:], acc[:])
                 else:
                     nc.scalar.copy(res[:], acc[:])
-                nc.sync.dma_start(out[ch, h * HALF : (h + 1) * HALF], res[:])
+                nc.sync.dma_start(out[ch, tok], res[:])
 
-        for h in range(HALVES):
-            form(h)
-            multiply(h)
+        seen = [0] * (T // P)
+        for what, j0, j1, b0, b1 in STEPS:
+            if what == "g":
+                h = b0 // 4
+                nc.vector.tensor_tensor(
+                    loss[:, j0, h * HALF : (h + 1) * HALF], book[j0][:].indirect(offsets[:, h * cols : (h + 1) * cols]), minus_beta[:], MULT
+                )
+                for b in range(b0, b1):
+                    if b in EARLY:
+                        add_turned(b, j0, loss)
+                continue
+            if what == "z":
+                for r0, r1 in runs(b0, b1, "S", 8):
+                    part = z[:, j0:j1, r0 * P : r1 * P]
+                    nc.scalar.activation(part, part, COPY, scale=BETA)
+                for r0, r1 in runs(b0, b1, "Z", 8):
+                    part = z[:, j0:j1, r0 * P : r1 * P]
+                    nc.vector.tensor_scalar(part, part, BETA, None, MULT)
+                for r0, r1 in runs(b0, b1, "EV", 4):
+                    part = loss[:, j0:j1, r0 * P : r1 * P]
+                    nc.vector.scalar_tensor_tensor(part, z[:, j0:j1, r0 * P : r1 * P], BETA, part, MULT, ADD)
+                for b in range(b0, b1):
+                    for j in range(j0, j1):
+                        if ROAD[b] == "E":
+                            add_turned(b, j, loss)
+                        elif ROAD[b] != "V":
+                            if b not in EARLY:
+                                add_turned(b, j, loss)
+                            add_turned(b, j, z)
+            elif what == "dy":
+                for b in range(b0, b1):
+                    for j in range(j0, j1):
+                        if ROAD[b] != "V":
+                            add_turned(b, j, dy)
+                for r0, r1 in runs(b0, b1, "V", ADDW):
+                    part = loss[:, j0:j1, r0 * P : r1 * P]
+                    nc.vector.tensor_tensor(part, part, dy[:, j0:j1, r0 * P : r1 * P], ADD)
+            elif what == "mm":
+                multiply(j0)
+                continue
+            for b in range(b0, b1):
+                seen[b] += j1 - j0
+            fresh = [b for b in range(b0, b1) if seen[b] == 2 * LANES]
+            while fresh:
+                last = fresh[0]
+                while last + 1 in fresh:
+                    last += 1
+                finish(fresh[0], last + 1)
+                fresh = [b for b in fresh if b > last]

@@ -25,25 +25,28 @@ LANES = 4
 HALF = 512
 PAIR = 256
 HALVES = T // HALF
-LOADS = [('cb', 1, 0, 0, 0), ('cb', 0, 0, 0, 0), ('cb', 3, 0, 0, 0), ('z', 0, 2, 0, 8), ('tw', 0, 0, 0, 0), ('ws', 0, 0, 0, 0), ('cb', 2, 0, 0, 0), ('z', 2, 4, 0, 8), ('dy', 2, 3, 0, 4), ('dy', 3, 4, 0, 3), ('dy', 0, 2, 0, 4), ('dy', 3, 4, 3, 6), ('dy', 1, 3, 4, 5), ('dy', 0, 1, 4, 6), ('dy', 1, 3, 5, 6), ('dy', 0, 2, 6, 8), ('dy', 2, 4, 6, 8), ('w', 0, 0, 0, 0)]
-STEPS = [('g', 1, 2, 0, 4), ('g', 1, 2, 4, 8), ('g', 0, 1, 0, 4), ('g', 0, 1, 4, 8), ('g', 3, 4, 0, 4), ('g', 2, 3, 0, 4), ('g', 3, 4, 4, 8), ('z', 0, 2, 0, 8), ('g', 2, 3, 4, 8), ('z', 2, 4, 0, 8), ('dy', 2, 3, 0, 4), ('dy', 3, 4, 0, 3), ('dy', 0, 2, 0, 4), ('dy', 3, 4, 3, 6), ('dy', 1, 3, 4, 5), ('mm', 0, 0, 0, 0), ('dy', 0, 1, 4, 6), ('dy', 1, 3, 5, 6), ('dy', 0, 2, 6, 8), ('dy', 2, 4, 6, 8), ('mm', 1, 0, 0, 0)]
-ROAD = 'VVZZSSVV'
+LOADS = [('cb', 0, 0, 0, 0), ('tw', 0, 0, 0, 0), ('ws', 0, 0, 0, 0), ('cb', 1, 0, 0, 0), ('cb', 2, 0, 0, 0), ('cb', 3, 0, 0, 0), ('z', 0, 2, 0, 8), ('z', 2, 4, 0, 8), ('dy', 0, 4, 0, 4), ('dy', 2, 4, 6, 8), ('dy', 0, 4, 4, 6), ('dy', 0, 2, 6, 8), ('w', 0, 0, 0, 0)]
+STEPS = [('g', 0, 1, 0, 4), ('g', 0, 1, 4, 8), ('g', 1, 2, 0, 4), ('g', 1, 2, 4, 8), ('g', 2, 3, 0, 4), ('g', 2, 3, 4, 8), ('g', 3, 4, 0, 4), ('g', 3, 4, 4, 8), ('z', 0, 2, 0, 8), ('z', 2, 4, 0, 8), ('dy', 0, 4, 0, 4), ('mm', 0, 0, 0, 0), ('dy', 2, 4, 6, 8), ('dy', 0, 2, 6, 8), ('dy', 0, 4, 4, 6), ('mm', 1, 0, 0, 0)]
+ROAD = 'WWSSSSWW'
 SCALE = 'SVSSSSVS'
-BACK = 'VVSSSSVS'
+BACK = 'VSSSSSVS'
 EMPTY = 'SSSSVSVS'
-EARLY = [3, 5]
-GIN = [1, 2, 0, 3, 4, 7, 3, 3]
-GROWS = [4, 4, 2, 5, 7, 0, 3, 5]
+EARLY = [2, 3, 4, 5]
+BSUM = [0, 0, 2, 3, 4, 5, 0, 0]
+BBACK = [0, 0, 0, 1, 6, 7, 0, 0]
+BACC = [2, 3, 0, 1, 4, 5, 6, 7]
+GIN = [0, 1, 2, 3, 4, 5, 6, 7]
+GROWS = [0, 1, 2, 3, 4, 5, 6, 7]
 MULW = 2
 ADDW = 4
-BACKW = 2
+BACKW = 1
 
 
 def tile_attend_gvq_sw_x_kernel(tc, zT, cb, dyT, tw, w_words, w_scales, offs, out):
     nc = tc.nc
     with ExitStack() as ctx:
         keep = ctx.enter_context(tc.tile_pool(name="keep", bufs=1))
-        psum = ctx.enter_context(tc.psum_pool(name="psum", bufs=8))
+        psum = ctx.enter_context(tc.psum_pool(name="psum", bufs=1))
 
         offsets = keep.tile([P, T // 16], U16, name="offsets")
         nc.sync.dma_start(offsets[:], offs)
@@ -77,14 +80,14 @@ def tile_attend_gvq_sw_x_kernel(tc, zT, cb, dyT, tw, w_words, w_scales, offs, ou
         minus_beta = keep.tile([P, HALF], F32, name="minus_beta")
         nc.vector.memset(minus_beta[:], -BETA)
 
-        tw_bank = psum.tile([P, 4, P], F32, name="bank")
+        tw_bank = psum.tile([P, 4, P], F32, name="bank7")
         nc.tensor.transpose(tw_bank[:, 0, :], tw_rows[:], ident[:])
         tw_cols = keep.tile([P, T // P], F32, name="tw_cols")
         nc.scalar.activation(tw_cols[:], tw_bank[:, 0, 0 : T // P], COPY)
         tw_wide = keep.tile([P, T], F32, name="tw_wide")
-        direct = [b for b in range(T // P) if ROAD[b] == "V"]
+        direct = [b for b in range(T // P) if ROAD[b] in "VW"]
         for k in range(0, len(direct), 4):
-            spread = psum.tile([P, 4, P], F32, name="bank")
+            spread = psum.tile([P, 4, P], F32, name="bank%d" % (6 + k // 4))
             for i, b in enumerate(direct[k : k + 4]):
                 nc.tensor.transpose(spread[:, i, :], tw_cols[:, b : b + 1].to_broadcast([P, P]), ident[:])
             for i, b in enumerate(direct[k : k + 4]):
@@ -98,7 +101,7 @@ def tile_attend_gvq_sw_x_kernel(tc, zT, cb, dyT, tw, w_words, w_scales, offs, ou
 
         def add_turned(b, j, source):
             if b not in sums:
-                sums[b] = psum.tile([P, LANES, P], F32, name="bank")
+                sums[b] = psum.tile([P, LANES, P], F32, name="bank%d" % BSUM[b])
                 turns[b] = 0
             turns[b] += 1
             total = (2 if ROAD[b] == "E" else 3) * LANES
@@ -121,7 +124,7 @@ def tile_attend_gvq_sw_x_kernel(tc, zT, cb, dyT, tw, w_words, w_scales, offs, ou
         def finish(b0, b1):
             g_rows = {}
             for b in range(b0, b1):
-                if ROAD[b] != "V":
+                if ROAD[b] not in "VW":
                     g_rows[b] = keep.tile([P, 2, P, 2], BF16, name="g_rows%d" % GROWS[b])
                     src = sums[b][:].rearrange("t (u e) p -> t u p e", e=2)
                     if SCALE[b] == "V":
@@ -138,10 +141,20 @@ def tile_attend_gvq_sw_x_kernel(tc, zT, cb, dyT, tw, w_words, w_scales, offs, ou
                         g_in[:, (s0 - r0) * P : (s1 - r0) * P, :], loss[:, :, tok].rearrange("p j t -> p t j"),
                         tw_wide[:, tok].unsqueeze(2).to_broadcast([P, (s1 - s0) * P, LANES]), MULT,
                     )
+            for r0, r1 in runs(b0, b1, "W", 2):
+                tok = slice(r0 * P, r1 * P)
+                flat = keep.tile([P, LANES, (r1 - r0) * P], BF16, name="flat%d" % r0)
+                nc.vector.tensor_tensor(
+                    flat[:], loss[:, :, tok], tw_wide[:, tok].unsqueeze(1).to_broadcast([P, LANES, (r1 - r0) * P]), MULT
+                )
+                g_in = keep.tile([P, (r1 - r0) * P, LANES], BF16, name="g_in%d" % GIN[r0], align_bytes=64)
+                made.append((g_in, r0, r1))
+                copy = nc.vector.tensor_copy if BACK[r0] == "V" else nc.scalar.copy
+                copy(g_in[:], flat[:].rearrange("p j t -> p t j"))
             for g_in, r0, r1 in made:
                 quantise(g_in, r0, r1)
             for r0, r1 in runs(b0, b1, "ESZ", BACKW):
-                back = psum.tile([P, 4, P], F32, name="bank")
+                back = psum.tile([P, 4, P], F32, name="bank%d" % BBACK[r0])
                 for b in range(r0, r1):
                     words = g_rows[b][:].rearrange("t u p e -> t (u p e)").bitcast(F32)
                     for u in range(2):
@@ -157,7 +170,7 @@ def tile_attend_gvq_sw_x_kernel(tc, zT, cb, dyT, tw, w_words, w_scales, offs, ou
         def multiply(h):
             tok = slice(h * HALF, (h + 1) * HALF)
             for m in range(D // P):
-                acc = psum.tile([P, HALF], F32, name="bank")
+                acc = psum.tile([P, HALF], F32, name="bank%d" % BACC[4 * h + m])
                 ch = slice(m * P, (m + 1) * P)
                 nc.tensor.matmul_mx(
                     out=acc[:], lhsT=w_code[:, ch].bitcast(E4M3X4), lhsT_scale=w_scale[:, ch],
@@ -188,23 +201,23 @@ def tile_attend_gvq_sw_x_kernel(tc, zT, cb, dyT, tw, w_words, w_scales, offs, ou
                 for r0, r1 in runs(b0, b1, "Z", 8):
                     part = z[:, j0:j1, r0 * P : r1 * P]
                     nc.vector.tensor_scalar(part, part, BETA, None, MULT)
-                for r0, r1 in runs(b0, b1, "EV", 4):
+                for r0, r1 in runs(b0, b1, "EVW", 4):
                     part = loss[:, j0:j1, r0 * P : r1 * P]
                     nc.vector.scalar_tensor_tensor(part, z[:, j0:j1, r0 * P : r1 * P], BETA, part, MULT, ADD)
                 for b in range(b0, b1):
                     for j in range(j0, j1):
                         if ROAD[b] == "E":
                             add_turned(b, j, loss)
-                        elif ROAD[b] != "V":
+                        elif ROAD[b] not in "VW":
                             if b not in EARLY:
                                 add_turned(b, j, loss)
                             add_turned(b, j, z)
             elif what == "dy":
                 for b in range(b0, b1):
                     for j in range(j0, j1):
-                        if ROAD[b] != "V":
+                        if ROAD[b] not in "VW":
                             add_turned(b, j, dy)
-                for r0, r1 in runs(b0, b1, "V", ADDW):
+                for r0, r1 in runs(b0, b1, "VW", ADDW):
                     part = loss[:, j0:j1, r0 * P : r1 * P]
                     nc.vector.tensor_tensor(part, part, dy[:, j0:j1, r0 * P : r1 * P], ADD)
             elif what == "mm":

@@ -18,6 +18,7 @@ E4M3X4 = mybir.dt.float8_e4m3fn_x4
 E5M2X4 = mybir.dt.float8_e5m2_x4
 MULT = mybir.AluOpType.mult
 ADD = mybir.AluOpType.add
+SUBTRACT = mybir.AluOpType.subtract
 COPY = mybir.ActivationFunctionType.Copy
 
 P = 128
@@ -77,8 +78,6 @@ def tile_attend_gvq_sw_x_kernel(tc, zT, cb, dyT, tw, w_words, w_scales, offs, ou
 
         ident = keep.tile([P, P], F32, name="ident")
         make_identity(nc, ident[:])
-        minus_beta = keep.tile([P, HALF], F32, name="minus_beta")
-        nc.vector.memset(minus_beta[:], -BETA)
 
         tw_bank = psum.tile([P, 4, P], F32, name="bank7")
         nc.tensor.transpose(tw_bank[:, 0, :], tw_rows[:], ident[:])
@@ -187,9 +186,10 @@ def tile_attend_gvq_sw_x_kernel(tc, zT, cb, dyT, tw, w_words, w_scales, offs, ou
         for what, j0, j1, b0, b1 in STEPS:
             if what == "g":
                 h = b0 // 4
-                nc.vector.tensor_tensor(
-                    loss[:, j0, h * HALF : (h + 1) * HALF], book[j0][:].indirect(offsets[:, h * cols : (h + 1) * cols]), minus_beta[:], MULT
-                )
+                nc.vector.tensor_copy(loss[:, j0, h * HALF : (h + 1) * HALF], book[j0][:].indirect(offsets[:, h * cols : (h + 1) * cols]))
+                for r0, r1 in runs(b0, b1, "SZ", 4):
+                    part = loss[:, j0, r0 * P : r1 * P]
+                    nc.scalar.activation(part, part, COPY, scale=-BETA)
                 for b in range(b0, b1):
                     if b in EARLY:
                         add_turned(b, j0, loss)
@@ -203,7 +203,10 @@ def tile_attend_gvq_sw_x_kernel(tc, zT, cb, dyT, tw, w_words, w_scales, offs, ou
                     nc.vector.tensor_scalar(part, part, BETA, None, MULT)
                 for r0, r1 in runs(b0, b1, "EVW", 4):
                     part = loss[:, j0:j1, r0 * P : r1 * P]
-                    nc.vector.scalar_tensor_tensor(part, z[:, j0:j1, r0 * P : r1 * P], BETA, part, MULT, ADD)
+                    nc.vector.tensor_tensor(part, z[:, j0:j1, r0 * P : r1 * P], part, SUBTRACT)
+                for r0, r1 in runs(b0, b1, "E", 4):
+                    part = loss[:, j0:j1, r0 * P : r1 * P]
+                    nc.scalar.activation(part, part, COPY, scale=BETA)
                 for b in range(b0, b1):
                     for j in range(j0, j1):
                         if ROAD[b] == "E":
@@ -219,7 +222,7 @@ def tile_attend_gvq_sw_x_kernel(tc, zT, cb, dyT, tw, w_words, w_scales, offs, ou
                             add_turned(b, j, dy)
                 for r0, r1 in runs(b0, b1, "VW", ADDW):
                     part = loss[:, j0:j1, r0 * P : r1 * P]
-                    nc.vector.tensor_tensor(part, part, dy[:, j0:j1, r0 * P : r1 * P], ADD)
+                    nc.vector.scalar_tensor_tensor(part, part, BETA, dy[:, j0:j1, r0 * P : r1 * P], MULT, ADD)
             elif what == "mm":
                 multiply(j0)
                 continue

@@ -18,29 +18,36 @@ E4M3X4 = mybir.dt.float8_e4m3fn_x4
 E5M2X4 = mybir.dt.float8_e5m2_x4
 MULT = mybir.AluOpType.mult
 ADD = mybir.AluOpType.add
-SUBTRACT = mybir.AluOpType.subtract
 COPY = mybir.ActivationFunctionType.Copy
 
 P = 128
 LANES = 4
 HALF = 512
-PAIR = 256
-HALVES = T // HALF
-LOADS = [('cb', 0, 0, 0, 0), ('tw', 0, 0, 0, 0), ('ws', 0, 0, 0, 0), ('cb', 1, 0, 0, 0), ('cb', 2, 0, 0, 0), ('cb', 3, 0, 0, 0), ('z', 0, 2, 0, 8), ('z', 2, 4, 0, 8), ('dy', 0, 4, 0, 4), ('dy', 2, 4, 6, 8), ('dy', 0, 4, 4, 6), ('dy', 0, 2, 6, 8), ('w', 0, 0, 0, 0)]
-STEPS = [('g', 0, 1, 0, 4), ('g', 0, 1, 4, 8), ('g', 1, 2, 0, 4), ('g', 1, 2, 4, 8), ('g', 2, 3, 0, 4), ('g', 2, 3, 4, 8), ('g', 3, 4, 0, 4), ('g', 3, 4, 4, 8), ('z', 0, 2, 0, 8), ('z', 2, 4, 0, 8), ('dy', 0, 4, 0, 4), ('mm', 0, 0, 0, 0), ('dy', 2, 4, 6, 8), ('dy', 0, 2, 6, 8), ('dy', 0, 4, 4, 6), ('mm', 1, 0, 0, 0)]
-ROAD = 'WWSSSSWW'
-SCALE = 'SVSSSSVS'
-BACK = 'VSSSSSVS'
-EMPTY = 'SSSSVSVS'
-EARLY = [2, 3, 4, 5]
-BSUM = [0, 0, 2, 3, 4, 5, 0, 0]
-BBACK = [0, 0, 0, 1, 6, 7, 0, 0]
-BACC = [2, 3, 0, 1, 4, 5, 6, 7]
-GIN = [0, 1, 2, 3, 4, 5, 6, 7]
-GROWS = [0, 1, 2, 3, 4, 5, 6, 7]
-MULW = 2
-ADDW = 4
-BACKW = 1
+BLOCKS = T // P
+BANKS = 8
+TERMS = 3
+
+ALL_LANES = range(LANES)
+LANE_PAIRS = (range(0, 2), range(2, 4))
+EARLY_LANES, LAST_LANE = range(0, LANES - 1), range(LANES - 1, LANES)
+FIRST_HALF, SECOND_HALF = range(0, 4), range(4, 8)
+DIRECT = range(4, 6)
+SECOND_TURNED = range(6, 8)
+LAST_LOADED, BEFORE_LAST = range(4, 5), range(5, 8)
+
+SCALED_ON_VECTOR = (0, 3)
+INTERLEAVED_ON_VECTOR = (0, 1)
+EMPTIED_ON_VECTOR = (3, 5, 7)
+
+TW_BANK, SPREAD_BANK = 7, 6
+
+
+def tokens(blocks):
+    return slice(blocks.start * P, blocks.stop * P)
+
+
+def span(lanes):
+    return slice(lanes.start, lanes.stop)
 
 
 def tile_attend_gvq_sw_x_kernel(tc, zT, cb, dyT, tw, w_words, w_scales, offs, out):
@@ -49,189 +56,167 @@ def tile_attend_gvq_sw_x_kernel(tc, zT, cb, dyT, tw, w_words, w_scales, offs, ou
         keep = ctx.enter_context(tc.tile_pool(name="keep", bufs=1))
         psum = ctx.enter_context(tc.psum_pool(name="psum", bufs=1))
 
+        def bank(number, shape):
+            return psum.tile(shape, F32, name="bank%d" % number)
+
         offsets = keep.tile([P, T // 16], U16, name="offsets")
         nc.sync.dma_start(offsets[:], offs)
 
         cb_lanes = cb.rearrange("(p j) c -> p j c", j=LANES)
-        lanes_of = {"z": zT.rearrange("(p j) t -> p j t", j=LANES), "dy": dyT.rearrange("(p j) t -> p j t", j=LANES)}
-        book = [keep.tile([P, C], F32, name="book%d" % j) for j in range(LANES)]
-        held = {"z": keep.tile([P, LANES, T], F32, name="z"), "dy": keep.tile([P, LANES, T], F32, name="dy")}
-        z, dy = held["z"], held["dy"]
+        z_lanes = zT.rearrange("(p j) t -> p j t", j=LANES)
+        dy_lanes = dyT.rearrange("(p j) t -> p j t", j=LANES)
+        book = [keep.tile([P, C], F32, name="book%d" % j) for j in ALL_LANES]
+        z = keep.tile([P, LANES, T], F32, name="z")
+        dy = keep.tile([P, LANES, T], F32, name="dy")
         w_code = keep.tile([P, D], U32, name="w_code", align_bytes=64)
         w_scale = keep.tile([P, D], U8, name="w_scale", align_bytes=64)
         tw_rows = keep.tile([P, P], F32, name="tw_rows")
         nc.gpsimd.memset(tw_rows[:], 0.0)
         nc.gpsimd.memset(w_scale[:].bitcast(I32), 0)
 
-        for what, j0, j1, b0, b1 in LOADS:
-            if what == "cb":
-                nc.sync.dma_start(book[j0][:], cb_lanes[:, j0, :])
-            elif what == "tw":
-                nc.sync.dma_start(tw_rows[0 : T // P, :], tw[0].rearrange("(b c) -> b c", c=P))
-            elif what == "w":
-                nc.sync.dma_start(w_code[:].bitcast(I32), w_words[0].rearrange("p n t -> p (n t)").bitcast(I32))
-            elif what == "ws":
-                for q in range(4):
-                    nc.scalar.dma_start(w_scale[32 * q : 32 * q + 4, :].bitcast(I32), w_scales[0, 4 * q : 4 * q + 4, :].bitcast(I32))
-            else:
-                nc.sync.dma_start(held[what][:, j0:j1, b0 * P : b1 * P], lanes_of[what][:, j0:j1, b0 * P : b1 * P])
+        def load(tile, source, lanes, blocks):
+            nc.sync.dma_start(tile[:, span(lanes), tokens(blocks)], source[:, span(lanes), tokens(blocks)])
+
+        nc.sync.dma_start(book[0][:], cb_lanes[:, 0, :])
+        nc.sync.dma_start(tw_rows[0:BLOCKS, :], tw[0].rearrange("(b c) -> b c", c=P))
+        for q in range(4):
+            nc.scalar.dma_start(
+                w_scale[32 * q : 32 * q + 4, :].bitcast(I32), w_scales[0, 4 * q : 4 * q + 4, :].bitcast(I32)
+            )
+        nc.sync.dma_start(book[1][:], cb_lanes[:, 1, :])
+        for lanes, j in zip(LANE_PAIRS, (2, 3)):
+            load(z, z_lanes, lanes, FIRST_HALF)
+            nc.sync.dma_start(book[j][:], cb_lanes[:, j, :])
+        for lanes in LANE_PAIRS:
+            load(dy, dy_lanes, lanes, FIRST_HALF)
+        nc.sync.dma_start(w_code[:].bitcast(I32), w_words[0].rearrange("p d j -> p (d j)").bitcast(I32))
+        for lanes in LANE_PAIRS:
+            load(z, z_lanes, lanes, SECOND_HALF)
+        for blocks in (BEFORE_LAST, LAST_LOADED):
+            load(dy, dy_lanes, ALL_LANES, blocks)
 
         ident = keep.tile([P, P], F32, name="ident")
         make_identity(nc, ident[:])
+        minus_beta = keep.tile([P, HALF], F32, name="minus_beta")
+        nc.vector.memset(minus_beta[:], -BETA)
 
-        tw_bank = psum.tile([P, 4, P], F32, name="bank7")
-        nc.tensor.transpose(tw_bank[:, 0, :], tw_rows[:], ident[:])
-        tw_cols = keep.tile([P, T // P], F32, name="tw_cols")
-        nc.scalar.activation(tw_cols[:], tw_bank[:, 0, 0 : T // P], COPY)
-        tw_wide = keep.tile([P, T], F32, name="tw_wide")
-        direct = [b for b in range(T // P) if ROAD[b] in "VW"]
-        for k in range(0, len(direct), 4):
-            spread = psum.tile([P, 4, P], F32, name="bank%d" % (6 + k // 4))
-            for i, b in enumerate(direct[k : k + 4]):
-                nc.tensor.transpose(spread[:, i, :], tw_cols[:, b : b + 1].to_broadcast([P, P]), ident[:])
-            for i, b in enumerate(direct[k : k + 4]):
-                nc.scalar.copy(tw_wide[:, b * P : (b + 1) * P], spread[:, i, :])
+        turned_tw = bank(TW_BANK, [P, P])
+        nc.tensor.transpose(turned_tw[:], tw_rows[:], ident[:])
+        tw_cols = keep.tile([P, BLOCKS], F32, name="tw_cols")
+        nc.scalar.activation(tw_cols[:], turned_tw[:, 0:BLOCKS], COPY)
+        spread = bank(SPREAD_BANK, [P, len(DIRECT), P])
+        for i, b in enumerate(DIRECT):
+            nc.tensor.transpose(spread[:, i, :], tw_cols[:, b : b + 1].to_broadcast([P, P]), ident[:])
+        tw_wide = keep.tile([P, len(DIRECT), P], F32, name="tw_wide")
+        nc.scalar.copy(tw_wide[:], spread[:])
 
-        loss = keep.tile([P, LANES, T], F32, name="loss")
+        partial = keep.tile([P, LANES, T], F32, name="partial")
         g_code = keep.tile([P, T], U32, name="g_code", align_bytes=64)
         g_scale = keep.tile([P, T], U8, name="g_scale", align_bytes=64)
-        cols = HALF // 16
-        sums, turns = {}, {}
+        sums, added = {}, {}
 
-        def add_turned(b, j, source):
-            if b not in sums:
-                sums[b] = psum.tile([P, LANES, P], F32, name="bank%d" % BSUM[b])
-                turns[b] = 0
-            turns[b] += 1
-            total = (2 if ROAD[b] == "E" else 3) * LANES
-            nc.tensor.matmul(sums[b][:, j, :], source[:, j, b * P : (b + 1) * P], ident[:], start=(turns[b] == 1), stop=(turns[b] == total), is_transpose=True)
-
-        def quantise(g_in, b0, b1):
-            tok = slice(b0 * P, b1 * P)
-            nc.vector.quantize_mx(out=g_code[:, tok].bitcast(E5M2X4), scales=g_scale[:, tok], in_=g_in[:].rearrange("p t j -> p (t j)"))
-
-        def runs(b0, b1, kinds, most):
-            found = []
-            for b in range(b0, b1):
-                if ROAD[b] in kinds:
-                    if found and found[-1][1] == b and b - found[-1][0] < most:
-                        found[-1][1] = b + 1
-                    else:
-                        found.append([b, b + 1])
-            return found
-
-        def finish(b0, b1):
-            g_rows = {}
-            for b in range(b0, b1):
-                if ROAD[b] not in "VW":
-                    g_rows[b] = keep.tile([P, 2, P, 2], BF16, name="g_rows%d" % GROWS[b])
-                    src = sums[b][:].rearrange("t (u e) p -> t u p e", e=2)
-                    if SCALE[b] == "V":
-                        nc.vector.tensor_scalar(g_rows[b][:], src, tw_cols[:, b : b + 1], None, MULT)
-                    else:
-                        nc.scalar.activation(g_rows[b][:], src, COPY, scale=tw_cols[:, b : b + 1])
-            made = []
-            for r0, r1 in runs(b0, b1, "V", 2):
-                g_in = keep.tile([P, (r1 - r0) * P, LANES], BF16, name="g_in%d" % GIN[r0], align_bytes=64)
-                made.append((g_in, r0, r1))
-                for s0, s1 in runs(r0, r1, "V", MULW):
-                    tok = slice(s0 * P, s1 * P)
-                    nc.vector.tensor_tensor(
-                        g_in[:, (s0 - r0) * P : (s1 - r0) * P, :], loss[:, :, tok].rearrange("p j t -> p t j"),
-                        tw_wide[:, tok].unsqueeze(2).to_broadcast([P, (s1 - s0) * P, LANES]), MULT,
+        def add_turned(source, lanes, blocks):
+            for b in blocks:
+                if b not in sums:
+                    sums[b] = bank(b, [P, LANES, P])
+                    added[b] = 0
+                for j in lanes:
+                    added[b] += 1
+                    nc.tensor.matmul(
+                        sums[b][:, j, :], source[:, j, b * P : (b + 1) * P], ident[:],
+                        start=(added[b] == 1), stop=(added[b] == TERMS * LANES), is_transpose=True,
                     )
-            for r0, r1 in runs(b0, b1, "W", 2):
-                tok = slice(r0 * P, r1 * P)
-                flat = keep.tile([P, LANES, (r1 - r0) * P], BF16, name="flat%d" % r0)
-                nc.vector.tensor_tensor(
-                    flat[:], loss[:, :, tok], tw_wide[:, tok].unsqueeze(1).to_broadcast([P, LANES, (r1 - r0) * P]), MULT
-                )
-                g_in = keep.tile([P, (r1 - r0) * P, LANES], BF16, name="g_in%d" % GIN[r0], align_bytes=64)
-                made.append((g_in, r0, r1))
-                copy = nc.vector.tensor_copy if BACK[r0] == "V" else nc.scalar.copy
-                copy(g_in[:], flat[:].rearrange("p j t -> p t j"))
-            for g_in, r0, r1 in made:
-                quantise(g_in, r0, r1)
-            for r0, r1 in runs(b0, b1, "ESZ", BACKW):
-                back = psum.tile([P, 4, P], F32, name="bank%d" % BBACK[r0])
-                for b in range(r0, r1):
-                    words = g_rows[b][:].rearrange("t u p e -> t (u p e)").bitcast(F32)
-                    for u in range(2):
-                        nc.tensor.transpose(back[:, 2 * (b - r0) + u, :], words[:, u * P : (u + 1) * P], ident[:])
-                g_in = keep.tile([P, (r1 - r0) * P, LANES], BF16, name="g_in%d" % GIN[r0], align_bytes=64)
-                copy = nc.vector.tensor_copy if BACK[r0] == "V" else nc.scalar.copy
-                copy(
-                    g_in[:].rearrange("p t j -> p (t j)").bitcast(F32).rearrange("p (b t u) -> p b t u", b=r1 - r0, u=2),
-                    back[:, 0 : 2 * (r1 - r0), :].rearrange("p (b u) t -> p b t u", u=2),
-                )
-                quantise(g_in, r0, r1)
 
-        def multiply(h):
-            tok = slice(h * HALF, (h + 1) * HALF)
-            for m in range(D // P):
-                acc = psum.tile([P, HALF], F32, name="bank%d" % BACC[4 * h + m])
-                ch = slice(m * P, (m + 1) * P)
-                nc.tensor.matmul_mx(
-                    out=acc[:], lhsT=w_code[:, ch].bitcast(E4M3X4), lhsT_scale=w_scale[:, ch],
-                    rhs=g_code[:, tok].bitcast(E5M2X4), rhs_scale=g_scale[:, tok], start=True, stop=True,
-                )
-                res = keep.tile([P, HALF], F32, name="res%d_%d" % (h, m))
-                if EMPTY[4 * h + m] == "V":
-                    nc.vector.tensor_copy(res[:], acc[:])
+        def scale_z(lanes, blocks):
+            piece = z[:, span(lanes), tokens(blocks)]
+            nc.scalar.activation(piece, piece, COPY, scale=BETA)
+
+        def quantise(g_in, b):
+            tok = slice(b * P, (b + 1) * P)
+            nc.vector.quantize_mx(
+                out=g_code[:, tok].bitcast(E5M2X4), scales=g_scale[:, tok], in_=g_in[:].rearrange("p t j -> p (t j)")
+            )
+
+        def scale_sums(blocks):
+            rows = {}
+            for b in blocks:
+                rows[b] = keep.tile([P, 2, P, 2], BF16, name="g_rows%d" % b)
+                source = sums[b][:].rearrange("t (u e) p -> t u p e", e=2)
+                if b in SCALED_ON_VECTOR:
+                    nc.vector.tensor_scalar(rows[b][:], source, tw_cols[:, b : b + 1], None, MULT)
                 else:
-                    nc.scalar.copy(res[:], acc[:])
-                nc.sync.dma_start(out[ch, tok], res[:])
+                    nc.scalar.activation(rows[b][:], source, COPY, scale=tw_cols[:, b : b + 1])
+            return rows
 
-        seen = [0] * (T // P)
-        for what, j0, j1, b0, b1 in STEPS:
-            if what == "g":
-                h = b0 // 4
-                nc.vector.tensor_copy(loss[:, j0, h * HALF : (h + 1) * HALF], book[j0][:].indirect(offsets[:, h * cols : (h + 1) * cols]))
-                for r0, r1 in runs(b0, b1, "SZ", 4):
-                    part = loss[:, j0, r0 * P : r1 * P]
-                    nc.scalar.activation(part, part, COPY, scale=-BETA)
-                for b in range(b0, b1):
-                    if b in EARLY:
-                        add_turned(b, j0, loss)
-                continue
-            if what == "z":
-                for r0, r1 in runs(b0, b1, "S", 8):
-                    part = z[:, j0:j1, r0 * P : r1 * P]
-                    nc.scalar.activation(part, part, COPY, scale=BETA)
-                for r0, r1 in runs(b0, b1, "Z", 8):
-                    part = z[:, j0:j1, r0 * P : r1 * P]
-                    nc.vector.tensor_scalar(part, part, BETA, None, MULT)
-                for r0, r1 in runs(b0, b1, "EVW", 4):
-                    part = loss[:, j0:j1, r0 * P : r1 * P]
-                    nc.vector.tensor_tensor(part, z[:, j0:j1, r0 * P : r1 * P], part, SUBTRACT)
-                for r0, r1 in runs(b0, b1, "E", 4):
-                    part = loss[:, j0:j1, r0 * P : r1 * P]
-                    nc.scalar.activation(part, part, COPY, scale=BETA)
-                for b in range(b0, b1):
-                    for j in range(j0, j1):
-                        if ROAD[b] == "E":
-                            add_turned(b, j, loss)
-                        elif ROAD[b] not in "VW":
-                            if b not in EARLY:
-                                add_turned(b, j, loss)
-                            add_turned(b, j, z)
-            elif what == "dy":
-                for b in range(b0, b1):
-                    for j in range(j0, j1):
-                        if ROAD[b] not in "VW":
-                            add_turned(b, j, dy)
-                for r0, r1 in runs(b0, b1, "VW", ADDW):
-                    part = loss[:, j0:j1, r0 * P : r1 * P]
-                    nc.vector.scalar_tensor_tensor(part, part, BETA, dy[:, j0:j1, r0 * P : r1 * P], MULT, ADD)
-            elif what == "mm":
-                multiply(j0)
-                continue
-            for b in range(b0, b1):
-                seen[b] += j1 - j0
-            fresh = [b for b in range(b0, b1) if seen[b] == 2 * LANES]
-            while fresh:
-                last = fresh[0]
-                while last + 1 in fresh:
-                    last += 1
-                finish(fresh[0], last + 1)
-                fresh = [b for b in fresh if b > last]
+        def turn_back(rows):
+            for b in rows:
+                back = bank(b, [P, 2, P])
+                words = rows[b][:].rearrange("t u p e -> t (u p e)").bitcast(F32)
+                for u in range(2):
+                    nc.tensor.transpose(back[:, u, :], words[:, u * P : (u + 1) * P], ident[:])
+                g_in = keep.tile([P, P, LANES], BF16, name="g_in%d" % b, align_bytes=64)
+                copy = nc.vector.tensor_copy if b in INTERLEAVED_ON_VECTOR else nc.scalar.copy
+                copy(
+                    g_in[:].rearrange("p t j -> p (t j)").bitcast(F32).rearrange("p (t u) -> p t u", u=2),
+                    back[:].rearrange("p u t -> p t u"),
+                )
+                quantise(g_in, b)
+
+        def add_dy_direct(b):
+            piece = partial[:, :, b * P : (b + 1) * P]
+            nc.vector.tensor_tensor(piece, piece, dy[:, :, b * P : (b + 1) * P], ADD)
+
+        def finish_direct(b):
+            g_in = keep.tile([P, P, LANES], BF16, name="g_in%d" % b, align_bytes=64)
+            nc.vector.tensor_tensor(
+                g_in[:], partial[:, :, b * P : (b + 1) * P].rearrange("p j t -> p t j"),
+                tw_wide[:, b - DIRECT.start, :].unsqueeze(2).to_broadcast([P, P, LANES]), MULT,
+            )
+            quantise(g_in, b)
+
+        columns = HALF // 16
+        for j in ALL_LANES:
+            for h, blocks in enumerate((FIRST_HALF, SECOND_HALF)):
+                listed = book[j][:].indirect(offsets[:, h * columns : (h + 1) * columns])
+                nc.vector.tensor_tensor(partial[:, j, tokens(blocks)], listed, minus_beta[:], MULT)
+
+        add_turned(partial, EARLY_LANES, FIRST_HALF)
+        add_turned(partial, EARLY_LANES, SECOND_TURNED)
+        for lanes in LANE_PAIRS:
+            scale_z(lanes, FIRST_HALF)
+            add_turned(z, lanes, FIRST_HALF)
+        for lanes in LANE_PAIRS:
+            add_turned(dy, lanes, FIRST_HALF)
+        add_turned(partial, LAST_LANE, FIRST_HALF)
+        turn_back(scale_sums(FIRST_HALF))
+
+        for lanes in LANE_PAIRS:
+            scale_z(lanes, SECOND_TURNED)
+            piece = partial[:, span(lanes), tokens(DIRECT)]
+            nc.vector.scalar_tensor_tensor(piece, z[:, span(lanes), tokens(DIRECT)], BETA, piece, MULT, ADD)
+            add_turned(z, lanes, SECOND_TURNED)
+        add_turned(partial, LAST_LANE, SECOND_TURNED)
+        add_turned(dy, ALL_LANES, SECOND_TURNED)
+        add_dy_direct(BEFORE_LAST.start)
+        rows = scale_sums(SECOND_TURNED)
+        finish_direct(BEFORE_LAST.start)
+        turn_back(rows)
+        add_dy_direct(LAST_LOADED.start)
+        finish_direct(LAST_LOADED.start)
+
+        for h, blocks in enumerate((FIRST_HALF, SECOND_HALF)):
+            for m in range(D // P):
+                number = h * (D // P) + m
+                product = bank((DIRECT.start + number) % BANKS, [P, HALF])
+                rows_d = slice(m * P, (m + 1) * P)
+                nc.tensor.matmul_mx(
+                    out=product[:], lhsT=w_code[:, rows_d].bitcast(E4M3X4), lhsT_scale=w_scale[:, rows_d],
+                    rhs=g_code[:, tokens(blocks)].bitcast(E5M2X4), rhs_scale=g_scale[:, tokens(blocks)],
+                    start=True, stop=True,
+                )
+                result = keep.tile([P, HALF], F32, name="result%d" % number)
+                if number in EMPTIED_ON_VECTOR:
+                    nc.vector.tensor_copy(result[:], product[:])
+                else:
+                    nc.scalar.copy(result[:], product[:])
+                nc.sync.dma_start(out[rows_d, tokens(blocks)], result[:])

from contextlib import ExitStack

import concourse.mybir as mybir
from concourse.masks import make_identity

T, C, D, DV = 1024, 2048, 512, 512
BETA = 0.25
FLOPS = 2 * DV * D * T
BYTES = 4 * (2 * DV * T + DV * C + T + D * T) + DV * D + 16 * D + 128 * (T // 16) * 2

F32 = mybir.dt.float32
BF16 = mybir.dt.bfloat16
I32 = mybir.dt.int32
U32 = mybir.dt.uint32
U16 = mybir.dt.uint16
U8 = mybir.dt.uint8
E4M3X4 = mybir.dt.float8_e4m3fn_x4
E5M2X4 = mybir.dt.float8_e5m2_x4
MULT = mybir.AluOpType.mult
ADD = mybir.AluOpType.add
COPY = mybir.ActivationFunctionType.Copy

P = 128
LANES = 4
HALF = 512
BLOCKS = T // P
BANKS = 8
TERMS = 3

ALL_LANES = range(LANES)
LANE_PAIRS = (range(0, 2), range(2, 4))
EARLY_LANES, LAST_LANE = range(0, LANES - 1), range(LANES - 1, LANES)
FIRST_HALF, SECOND_HALF = range(0, 4), range(4, 8)
DIRECT = range(4, 6)
SECOND_TURNED = range(6, 8)
LAST_LOADED, BEFORE_LAST = range(4, 5), range(5, 8)

SCALED_ON_VECTOR = (0, 3)
INTERLEAVED_ON_VECTOR = (0, 1)
EMPTIED_ON_VECTOR = (3, 5, 7)

TW_BANK, SPREAD_BANK = 7, 6


def tokens(blocks):
    return slice(blocks.start * P, blocks.stop * P)


def span(lanes):
    return slice(lanes.start, lanes.stop)


def tile_attend_gvq_sw_x_kernel(tc, zT, cb, dyT, tw, w_words, w_scales, offs, out):
    nc = tc.nc
    with ExitStack() as ctx:
        keep = ctx.enter_context(tc.tile_pool(name="keep", bufs=1))
        psum = ctx.enter_context(tc.psum_pool(name="psum", bufs=1))

        def bank(number, shape):
            return psum.tile(shape, F32, name="bank%d" % number)

        offsets = keep.tile([P, T // 16], U16, name="offsets")
        nc.sync.dma_start(offsets[:], offs)

        cb_lanes = cb.rearrange("(p j) c -> p j c", j=LANES)
        z_lanes = zT.rearrange("(p j) t -> p j t", j=LANES)
        dy_lanes = dyT.rearrange("(p j) t -> p j t", j=LANES)
        book = [keep.tile([P, C], F32, name="book%d" % j) for j in ALL_LANES]
        z = keep.tile([P, LANES, T], F32, name="z")
        dy = keep.tile([P, LANES, T], F32, name="dy")
        w_code = keep.tile([P, D], U32, name="w_code", align_bytes=64)
        w_scale = keep.tile([P, D], U8, name="w_scale", align_bytes=64)
        tw_rows = keep.tile([P, P], F32, name="tw_rows")
        nc.gpsimd.memset(tw_rows[:], 0.0)
        nc.gpsimd.memset(w_scale[:].bitcast(I32), 0)

        def load(tile, source, lanes, blocks):
            nc.sync.dma_start(tile[:, span(lanes), tokens(blocks)], source[:, span(lanes), tokens(blocks)])

        nc.sync.dma_start(book[0][:], cb_lanes[:, 0, :])
        nc.sync.dma_start(tw_rows[0:BLOCKS, :], tw[0].rearrange("(b c) -> b c", c=P))
        for q in range(4):
            nc.scalar.dma_start(
                w_scale[32 * q : 32 * q + 4, :].bitcast(I32), w_scales[0, 4 * q : 4 * q + 4, :].bitcast(I32)
            )
        nc.sync.dma_start(book[1][:], cb_lanes[:, 1, :])
        for lanes, j in zip(LANE_PAIRS, (2, 3)):
            load(z, z_lanes, lanes, FIRST_HALF)
            nc.sync.dma_start(book[j][:], cb_lanes[:, j, :])
        for lanes in LANE_PAIRS:
            load(dy, dy_lanes, lanes, FIRST_HALF)
        nc.sync.dma_start(w_code[:].bitcast(I32), w_words[0].rearrange("p d j -> p (d j)").bitcast(I32))
        for lanes in LANE_PAIRS:
            load(z, z_lanes, lanes, SECOND_HALF)
        for blocks in (BEFORE_LAST, LAST_LOADED):
            load(dy, dy_lanes, ALL_LANES, blocks)

        ident = keep.tile([P, P], F32, name="ident")
        make_identity(nc, ident[:])
        minus_beta = keep.tile([P, HALF], F32, name="minus_beta")
        nc.vector.memset(minus_beta[:], -BETA)

        turned_tw = bank(TW_BANK, [P, P])
        nc.tensor.transpose(turned_tw[:], tw_rows[:], ident[:])
        tw_cols = keep.tile([P, BLOCKS], F32, name="tw_cols")
        nc.scalar.activation(tw_cols[:], turned_tw[:, 0:BLOCKS], COPY)
        spread = bank(SPREAD_BANK, [P, len(DIRECT), P])
        for i, b in enumerate(DIRECT):
            nc.tensor.transpose(spread[:, i, :], tw_cols[:, b : b + 1].to_broadcast([P, P]), ident[:])
        tw_wide = keep.tile([P, len(DIRECT), P], F32, name="tw_wide")
        nc.scalar.copy(tw_wide[:], spread[:])

        partial = keep.tile([P, LANES, T], F32, name="partial")
        g_code = keep.tile([P, T], U32, name="g_code", align_bytes=64)
        g_scale = keep.tile([P, T], U8, name="g_scale", align_bytes=64)
        sums, added = {}, {}

        def add_turned(source, lanes, blocks):
            for b in blocks:
                if b not in sums:
                    sums[b] = bank(b, [P, LANES, P])
                    added[b] = 0
                for j in lanes:
                    added[b] += 1
                    nc.tensor.matmul(
                        sums[b][:, j, :], source[:, j, b * P : (b + 1) * P], ident[:],
                        start=(added[b] == 1), stop=(added[b] == TERMS * LANES), is_transpose=True,
                    )

        def scale_z(lanes, blocks):
            piece = z[:, span(lanes), tokens(blocks)]
            nc.scalar.activation(piece, piece, COPY, scale=BETA)

        def quantise(g_in, b):
            tok = slice(b * P, (b + 1) * P)
            nc.vector.quantize_mx(
                out=g_code[:, tok].bitcast(E5M2X4), scales=g_scale[:, tok], in_=g_in[:].rearrange("p t j -> p (t j)")
            )

        def scale_sums(blocks):
            rows = {}
            for b in blocks:
                rows[b] = keep.tile([P, 2, P, 2], BF16, name="g_rows%d" % b)
                source = sums[b][:].rearrange("t (u e) p -> t u p e", e=2)
                if b in SCALED_ON_VECTOR:
                    nc.vector.tensor_scalar(rows[b][:], source, tw_cols[:, b : b + 1], None, MULT)
                else:
                    nc.scalar.activation(rows[b][:], source, COPY, scale=tw_cols[:, b : b + 1])
            return rows

        def turn_back(rows):
            for b in rows:
                back = bank(b, [P, 2, P])
                words = rows[b][:].rearrange("t u p e -> t (u p e)").bitcast(F32)
                for u in range(2):
                    nc.tensor.transpose(back[:, u, :], words[:, u * P : (u + 1) * P], ident[:])
                g_in = keep.tile([P, P, LANES], BF16, name="g_in%d" % b, align_bytes=64)
                copy = nc.vector.tensor_copy if b in INTERLEAVED_ON_VECTOR else nc.scalar.copy
                copy(
                    g_in[:].rearrange("p t j -> p (t j)").bitcast(F32).rearrange("p (t u) -> p t u", u=2),
                    back[:].rearrange("p u t -> p t u"),
                )
                quantise(g_in, b)

        def add_dy_direct(b):
            piece = partial[:, :, b * P : (b + 1) * P]
            nc.vector.tensor_tensor(piece, piece, dy[:, :, b * P : (b + 1) * P], ADD)

        def finish_direct(b):
            g_in = keep.tile([P, P, LANES], BF16, name="g_in%d" % b, align_bytes=64)
            nc.vector.tensor_tensor(
                g_in[:], partial[:, :, b * P : (b + 1) * P].rearrange("p j t -> p t j"),
                tw_wide[:, b - DIRECT.start, :].unsqueeze(2).to_broadcast([P, P, LANES]), MULT,
            )
            quantise(g_in, b)

        columns = HALF // 16
        for j in ALL_LANES:
            for h, blocks in enumerate((FIRST_HALF, SECOND_HALF)):
                listed = book[j][:].indirect(offsets[:, h * columns : (h + 1) * columns])
                nc.vector.tensor_tensor(partial[:, j, tokens(blocks)], listed, minus_beta[:], MULT)

        add_turned(partial, EARLY_LANES, FIRST_HALF)
        add_turned(partial, EARLY_LANES, SECOND_TURNED)
        for lanes in LANE_PAIRS:
            scale_z(lanes, FIRST_HALF)
            add_turned(z, lanes, FIRST_HALF)
        for lanes in LANE_PAIRS:
            add_turned(dy, lanes, FIRST_HALF)
        add_turned(partial, LAST_LANE, FIRST_HALF)
        turn_back(scale_sums(FIRST_HALF))

        for lanes in LANE_PAIRS:
            scale_z(lanes, SECOND_TURNED)
            piece = partial[:, span(lanes), tokens(DIRECT)]
            nc.vector.scalar_tensor_tensor(piece, z[:, span(lanes), tokens(DIRECT)], BETA, piece, MULT, ADD)
            add_turned(z, lanes, SECOND_TURNED)
        add_turned(partial, LAST_LANE, SECOND_TURNED)
        add_turned(dy, ALL_LANES, SECOND_TURNED)
        add_dy_direct(BEFORE_LAST.start)
        rows = scale_sums(SECOND_TURNED)
        finish_direct(BEFORE_LAST.start)
        turn_back(rows)
        add_dy_direct(LAST_LOADED.start)
        finish_direct(LAST_LOADED.start)

        for h, blocks in enumerate((FIRST_HALF, SECOND_HALF)):
            for m in range(D // P):
                number = h * (D // P) + m
                product = bank((DIRECT.start + number) % BANKS, [P, HALF])
                rows_d = slice(m * P, (m + 1) * P)
                nc.tensor.matmul_mx(
                    out=product[:], lhsT=w_code[:, rows_d].bitcast(E4M3X4), lhsT_scale=w_scale[:, rows_d],
                    rhs=g_code[:, tokens(blocks)].bitcast(E5M2X4), rhs_scale=g_scale[:, tokens(blocks)],
                    start=True, stop=True,
                )
                result = keep.tile([P, HALF], F32, name="result%d" % number)
                if number in EMPTIED_ON_VECTOR:
                    nc.vector.tensor_copy(result[:], product[:])
                else:
                    nc.scalar.copy(result[:], product[:])
                nc.sync.dma_start(out[rows_d, tokens(blocks)], result[:])
